import numpy as np
import ml_dtypes


def mxq(x, axis, fmt="e4m3"):
    dtype, down = {"e4m3": (ml_dtypes.float8_e4m3fn, 7), "e5m2": (ml_dtypes.float8_e5m2, 14)}[fmt]
    v = np.moveaxis(np.asarray(x, np.float32).astype(ml_dtypes.bfloat16).astype(np.float64), axis, -1)
    blocks = v.reshape(v.shape[:-1] + (-1, 32))
    amax = np.abs(blocks).max(-1, keepdims=True)
    byte = np.maximum(np.where(amax > 0, np.frexp(amax)[1] - 1 + 127, 0) - down, 1)
    scale = np.exp2(byte - 127.0)
    codes = (blocks / scale).astype(np.float32).astype(dtype).astype(np.float64)
    return np.moveaxis((codes * scale).reshape(v.shape), -1, axis)


WIDE = False


def mx_kscale(k, group=512):
    if not WIDE:
        return np.ones(k)
    levels = np.array([18, -18])
    if group != 512:
        return np.exp2(np.random.permutation(np.resize(levels, k // group))).repeat(group)
    if k % 512:
        return np.exp2(np.random.permutation(np.resize(levels, k // 32))).repeat(32)
    a = np.empty((k // 512, 16))
    for p in range(k // 512):
        a[p, :8] = np.random.permutation(np.resize(levels, 8))
        for g in range(8):
            far = levels[np.abs(levels - a[p, g]) >= 10]
            a[p, g + 8] = far[np.random.randint(len(far))]
    return np.exp2(a.ravel()).repeat(32)


def f64(x):
    return np.asarray(x).astype(np.float64)


G, D, I, F, E = 8, 128, 128, 128, 128


def sgn(shape):
    return np.random.uniform(0.5, 2.0, shape) * np.where(np.random.standard_normal(shape) < 0, -1.0, 1.0)


def setup_inputs():
    n = np.random.standard_normal
    s_d = mx_kscale(D, 0)
    s_i = mx_kscale(I, 0)
    return {
        "kT": (n((G, D, I)) / np.sqrt(D) / s_d[:, None]).astype(np.float32),
        "S": (n((G, D, E)) * s_d[:, None]).astype(np.float32),
        "v": (n((G, I, E))).astype(np.float32),
        "be": (sgn((G, I, 1)) * s_i[:, None]).astype(np.float32),
        "kn": (n((G, I, F)) / np.sqrt(I) / s_i[:, None] * s_d).astype(np.float32),
        "al": (np.random.uniform(0.9, 1.0, (G, F, 1))).astype(np.float32),
    }


def reference(kT, S, v, be, kn, al):
    kTq = mxq(f64(kT), 1, "e4m3")
    Sq = mxq(f64(S), 1, "e4m3")
    z = kTq.transpose(0, 2, 1) @ Sq
    u = (z - f64(v)) * f64(be)
    knq = mxq(f64(kn), 1, "e4m3")
    uq = mxq(u, 1, "e4m3")
    w = knq.transpose(0, 2, 1) @ uq
    o = f64(al) * f64(S) - w
    return o

@@ -1,0 +1,143 @@
+from contextlib import ExitStack
+
+import concourse.mybir as mybir
+
+G, D = 8, 128
+FLOPS = 2 * 2 * G * D * D * D
+
+F32 = mybir.dt.float32
+BF16 = mybir.dt.bfloat16
+U32 = mybir.dt.uint32
+U8 = mybir.dt.uint8
+FP8X4 = mybir.dt.float8_e4m3fn_x4
+ALU = mybir.AluOpType
+COPY = mybir.ActivationFunctionType.Copy
+
+P = 128
+PACK = 4
+ROWS = 32
+TILES = 4
+SETS = 2
+RUN = 4
+
+
+def interleaved(dst, src):
+    return (
+        dst.rearrange("p (c i) t -> p c t i", i=RUN),
+        src.rearrange("p t (c i) -> p c t i", i=RUN),
+    )
+
+
+def tile_rows_upd_ttt_kernel(tc, kT, S, v, be, kn, al, out):
+    nc = tc.nc
+    with ExitStack() as ctx:
+        sb = ctx.enter_context(tc.tile_pool(name="sb", bufs=1))
+        ps = ctx.enter_context(tc.psum_pool(name="ps", bufs=1))
+        ctx.enter_context(tc.manual_schedule())
+
+        def rows_of(x):
+            return x.rearrange("(s c) (p j) n -> (c p) s (j n)", s=SETS, j=PACK)
+
+        def sbuf(name, shape, dtype):
+            return sb.tile(shape, dtype, name=name, align_bytes=64)
+
+        def cast(engine, dst, src):
+            o, i = interleaved(dst, src)
+            if engine is nc.scalar:
+                nc.scalar.activation(out=o, in_=i, func=COPY)
+            else:
+                nc.vector.tensor_copy(out=o, in_=i)
+
+        def quantize(name, words):
+            codes = sbuf(name + "_codes", [P, D], U32)
+            scales = sbuf(name + "_scales", [P, D], U8)
+            nc.vector.quantize_mx(out=codes[:].bitcast(FP8X4), scales=scales[:],
+                                  in_=words[:].rearrange("p n j -> p (n j)"))
+            return codes, scales
+
+        def product(dst, c, lhs, rhs):
+            r = slice(ROWS * c, ROWS * (c + 1))
+            nc.tensor.matmul_mx(out=dst, lhsT=lhs[0][r, :].bitcast(FP8X4), lhsT_scale=lhs[1][r, :],
+                                rhs=rhs[0][r, :].bitcast(FP8X4), rhs_scale=rhs[1][r, :],
+                                start=True, stop=True)
+
+        kT_raw, S_raw, v_raw = [], [], []
+        for s in range(SETS):
+            kT_raw.append(sbuf("kT_raw%d" % s, [P, PACK, D], F32))
+            nc.sync.dma_start(out=kT_raw[s][:].rearrange("p j n -> p (j n)"), in_=rows_of(kT)[:, s, :])
+            S_raw.append(sbuf("S_raw%d" % s, [P, PACK, D], F32))
+            nc.sync.dma_start(out=S_raw[s][:].rearrange("p j n -> p (j n)"), in_=rows_of(S)[:, s, :])
+        for s in range(SETS):
+            v_raw.append(sbuf("v_raw%d" % s, [P, TILES, D], F32))
+            nc.sync.dma_start(out=v_raw[s][:], in_=v[TILES * s : TILES * (s + 1)].rearrange("g i e -> i g e"))
+        kn_raw = sbuf("kn_raw", [P, SETS, PACK * D], F32)
+        nc.sync.dma_start(out=kn_raw[:], in_=rows_of(kn))
+        S_out = sbuf("S_out", [P, G, D], F32)
+        nc.sync.dma_start(out=S_out[:], in_=S.rearrange("g f e -> f g e"))
+
+        small = {}
+        for name, x in (("be", be), ("al", al)):
+            t = sbuf(name + "_rows", [P, G * ROWS], F32)
+            nc.gpsimd.memset(t[:], 0.0)
+            nc.gpsimd.dma_start(out=t[0:P:ROWS, :].rearrange("q (g r) -> q g r", g=G),
+                                in_=x.rearrange("g (q r) o -> q g (r o)", r=ROWS))
+            small[name] = t
+
+        def columns(name):
+            t = sbuf(name + "_cols", [P, G * ROWS], F32)
+            nc.vector.transpose(out=t[:], in_=small[name][:])
+            return [t[:, ROWS * g : ROWS * g + 1] for g in range(G)]
+
+        banks = {}
+        for s in range(SETS):
+            for c in range(TILES):
+                banks[s, c] = ps.tile([P, 512], F32, name="bank%d%d" % (s, c))
+
+        be_col = None
+        for s in range(SETS):
+            kT_w = sbuf("kT_w%d" % s, [P, D, PACK], BF16)
+            cast(nc.scalar, kT_w[:], kT_raw[s][:])
+            S_w = sbuf("S_w%d" % s, [P, D, PACK], BF16)
+            cast(nc.vector, S_w[:], S_raw[s][:])
+            kT_q = quantize("kT%d" % s, kT_w)
+            S_q = quantize("S%d" % s, S_w)
+            for c in range(TILES):
+                product(banks[s, c][:, 0:D], c, kT_q, S_q)
+            if s == 0:
+                be_col = columns("be")
+
+        u_tok = [sbuf("u_tok%d" % c, [P, SETS, D], BF16) for c in range(TILES)]
+        u_rows = sbuf("u_rows", [P, PACK, SETS, D], BF16)
+        for s in range(SETS):
+            for c in range(TILES):
+                g = TILES * s + c
+                vb = sbuf("vb%d" % g, [P, D], F32)
+                nc.scalar.activation(out=vb[:], in_=v_raw[s][:, c, :], func=COPY, scale=be_col[g])
+                nc.vector.scalar_tensor_tensor(out=u_tok[c][:, s, :], in0=banks[s, c][:, 0:D], scalar=be_col[g],
+                                               in1=vb[:], op0=ALU.mult, op1=ALU.subtract)
+        for c in range(TILES):
+            nc.scalar.dma_start(out=u_rows[ROWS * c : ROWS * (c + 1)].rearrange("p j s e -> p j (s e)"),
+                                in_=u_tok[c][:].rearrange("i s e -> i (s e)"))
+
+        al_col = columns("al")
+        kn_w = [sbuf("kn_w%d" % s, [P, D, PACK], BF16) for s in range(SETS)]
+        cast(nc.vector, kn_w[0][:], kn_raw[:, 0, :].rearrange("p (j n) -> p j n", j=PACK))
+        cast(nc.scalar, kn_w[1][:], kn_raw[:, 1, :].rearrange("p (j n) -> p j n", j=PACK))
+        kn_q = [quantize("kn%d" % s, kn_w[s]) for s in range(SETS)]
+
+        u_w = [sbuf("u_w%d" % s, [P, D, PACK], BF16) for s in range(SETS)]
+        cast(nc.vector, u_w[0][:], u_rows[:, :, 0, :])
+        cast(nc.scalar, u_w[1][:], u_rows[:, :, 1, :])
+        for s in range(SETS):
+            u_q = quantize("u%d" % s, u_w[s])
+            for c in range(TILES):
+                product(banks[s, c][:, D : 2 * D], c, kn_q[s], u_q)
+
+        for pair in range(G // 2):
+            res = sbuf("res%d" % pair, [P, 2, D], F32)
+            for h in range(2):
+                g = 2 * pair + h
+                nc.vector.scalar_tensor_tensor(out=res[:, h, :], in0=S_out[:, g, :], scalar=al_col[g],
+                                               in1=banks[divmod(g, TILES)][:, D : 2 * D],
+                                               op0=ALU.mult, op1=ALU.subtract)
+            nc.sync.dma_start(out=out[2 * pair : 2 * pair + 2].rearrange("g f e -> f g e"), in_=res[:])

@@ -61,12 +61,19 @@ def tile_rows_upd_ttt_kernel(tc, kT, S, v, be, kn, al, out):
                                 rhs=rhs[0][r, :].bitcast(FP8X4), rhs_scale=rhs[1][r, :],
                                 start=True, stop=True)
 
+        small = sbuf("small_rows", [P, G * ROWS], F32)
+        nc.vector.memset(small[:], 0.0)
+
         kT_raw, S_raw, v_raw = [], [], []
         for s in range(SETS):
             kT_raw.append(sbuf("kT_raw%d" % s, [P, PACK, D], F32))
             nc.sync.dma_start(out=kT_raw[s][:].rearrange("p j n -> p (j n)"), in_=rows_of(kT)[:, s, :])
             S_raw.append(sbuf("S_raw%d" % s, [P, PACK, D], F32))
             nc.sync.dma_start(out=S_raw[s][:].rearrange("p j n -> p (j n)"), in_=rows_of(S)[:, s, :])
+            if s == 0:
+                for r, x in enumerate((be, al)):
+                    nc.sync.dma_start(out=small[r:P:ROWS, :].rearrange("q (g r) -> q g r", g=G),
+                                      in_=x.rearrange("g (q r) o -> q g (r o)", r=ROWS))
         for s in range(SETS):
             v_raw.append(sbuf("v_raw%d" % s, [P, TILES, D], F32))
             nc.sync.dma_start(out=v_raw[s][:], in_=v[TILES * s : TILES * (s + 1)].rearrange("g i e -> i g e"))
@@ -75,25 +82,14 @@ def tile_rows_upd_ttt_kernel(tc, kT, S, v, be, kn, al, out):
         S_out = sbuf("S_out", [P, G, D], F32)
         nc.sync.dma_start(out=S_out[:], in_=S.rearrange("g f e -> f g e"))
 
-        small = {}
-        for name, x in (("be", be), ("al", al)):
-            t = sbuf(name + "_rows", [P, G * ROWS], F32)
-            nc.gpsimd.memset(t[:], 0.0)
-            nc.gpsimd.dma_start(out=t[0:P:ROWS, :].rearrange("q (g r) -> q g r", g=G),
-                                in_=x.rearrange("g (q r) o -> q g (r o)", r=ROWS))
-            small[name] = t
-
-        def columns(name):
-            t = sbuf(name + "_cols", [P, G * ROWS], F32)
-            nc.vector.transpose(out=t[:], in_=small[name][:])
-            return [t[:, ROWS * g : ROWS * g + 1] for g in range(G)]
-
         banks = {}
         for s in range(SETS):
             for c in range(TILES):
                 banks[s, c] = ps.tile([P, 512], F32, name="bank%d%d" % (s, c))
 
-        be_col = None
+        cols = sbuf("small_cols", [P, G * ROWS], F32)
+        be_col = [cols[:, ROWS * g : ROWS * g + 1] for g in range(G)]
+        al_col = [cols[:, ROWS * g + 1 : ROWS * g + 2] for g in range(G)]
         for s in range(SETS):
             kT_w = sbuf("kT_w%d" % s, [P, D, PACK], BF16)
             cast(nc.scalar, kT_w[:], kT_raw[s][:])
@@ -104,7 +100,7 @@ def tile_rows_upd_ttt_kernel(tc, kT, S, v, be, kn, al, out):
             for c in range(TILES):
                 product(banks[s, c][:, 0:D], c, kT_q, S_q)
             if s == 0:
-                be_col = columns("be")
+                nc.vector.transpose(out=cols[:], in_=small[:])
 
         u_tok = [sbuf("u_tok%d" % c, [P, SETS, D], BF16) for c in range(TILES)]
         u_rows = sbuf("u_rows", [P, PACK, SETS, D], BF16)
@@ -119,7 +115,6 @@ def tile_rows_upd_ttt_kernel(tc, kT, S, v, be, kn, al, out):
             nc.scalar.dma_start(out=u_rows[ROWS * c : ROWS * (c + 1)].rearrange("p j s e -> p j (s e)"),
                                 in_=u_tok[c][:].rearrange("i s e -> i (s e)"))
 
-        al_col = columns("al")
         kn_w = [sbuf("kn_w%d" % s, [P, D, PACK], BF16) for s in range(SETS)]
         cast(nc.vector, kn_w[0][:], kn_raw[:, 0, :].rearrange("p (j n) -> p j n", j=PACK))
         cast(nc.scalar, kn_w[1][:], kn_raw[:, 1, :].rearrange("p (j n) -> p j n", j=PACK))

@@ -19,6 +19,7 @@ ROWS = 32
 TILES = 4
 SETS = 2
 RUN = 4
+ORDER = (0, 2, 1, 3)
 
 
 def interleaved(dst, src):
@@ -77,10 +78,8 @@ def tile_rows_upd_ttt_kernel(tc, kT, S, v, be, kn, al, out):
         for s in range(SETS):
             v_raw.append(sbuf("v_raw%d" % s, [P, TILES, D], F32))
             nc.sync.dma_start(out=v_raw[s][:], in_=v[TILES * s : TILES * (s + 1)].rearrange("g i e -> i g e"))
-        kn_raw = sbuf("kn_raw", [P, SETS, PACK * D], F32)
-        nc.sync.dma_start(out=kn_raw[:], in_=rows_of(kn))
-        S_out = sbuf("S_out", [P, G, D], F32)
-        nc.sync.dma_start(out=S_out[:], in_=S.rearrange("g f e -> f g e"))
+        kn_raw = [sbuf("kn_raw%d" % s, [P, PACK, D], F32) for s in range(SETS)]
+        nc.sync.dma_start(out=kn_raw[0][:].rearrange("p j n -> p (j n)"), in_=rows_of(kn)[:, 0, :])
 
         banks = {}
         for s in range(SETS):
@@ -102,37 +101,40 @@ def tile_rows_upd_ttt_kernel(tc, kT, S, v, be, kn, al, out):
             if s == 0:
                 nc.vector.transpose(out=cols[:], in_=small[:])
 
-        u_tok = [sbuf("u_tok%d" % c, [P, SETS, D], BF16) for c in range(TILES)]
-        u_rows = sbuf("u_rows", [P, PACK, SETS, D], BF16)
+        u_rows = [sbuf("u_rows%d" % s, [P, PACK, D], BF16) for s in range(SETS)]
         for s in range(SETS):
-            for c in range(TILES):
+            for c in ORDER:
                 g = TILES * s + c
                 vb = sbuf("vb%d" % g, [P, D], F32)
                 nc.scalar.activation(out=vb[:], in_=v_raw[s][:, c, :], func=COPY, scale=be_col[g])
-                nc.vector.scalar_tensor_tensor(out=u_tok[c][:, s, :], in0=banks[s, c][:, 0:D], scalar=be_col[g],
+                u_tok = sbuf("u_tok%d" % g, [P, D], BF16)
+                nc.vector.scalar_tensor_tensor(out=u_tok[:], in0=banks[s, c][:, 0:D], scalar=be_col[g],
                                                in1=vb[:], op0=ALU.mult, op1=ALU.subtract)
-        for c in range(TILES):
-            nc.scalar.dma_start(out=u_rows[ROWS * c : ROWS * (c + 1)].rearrange("p j s e -> p j (s e)"),
-                                in_=u_tok[c][:].rearrange("i s e -> i (s e)"))
+                nc.sync.dma_start(out=u_rows[s][ROWS * c : ROWS * (c + 1)], in_=u_tok[:])
+            if s == 0:
+                nc.sync.dma_start(out=kn_raw[1][:].rearrange("p j n -> p (j n)"), in_=rows_of(kn)[:, 1, :])
 
-        kn_w = [sbuf("kn_w%d" % s, [P, D, PACK], BF16) for s in range(SETS)]
-        cast(nc.vector, kn_w[0][:], kn_raw[:, 0, :].rearrange("p (j n) -> p j n", j=PACK))
-        cast(nc.scalar, kn_w[1][:], kn_raw[:, 1, :].rearrange("p (j n) -> p j n", j=PACK))
-        kn_q = [quantize("kn%d" % s, kn_w[s]) for s in range(SETS)]
-
-        u_w = [sbuf("u_w%d" % s, [P, D, PACK], BF16) for s in range(SETS)]
-        cast(nc.vector, u_w[0][:], u_rows[:, :, 0, :])
-        cast(nc.scalar, u_w[1][:], u_rows[:, :, 1, :])
+        S_out = []
         for s in range(SETS):
-            u_q = quantize("u%d" % s, u_w[s])
-            for c in range(TILES):
-                product(banks[s, c][:, D : 2 * D], c, kn_q[s], u_q)
+            S_out.append(sbuf("S_out%d" % s, [P, TILES, D], F32))
+            nc.sync.dma_start(out=S_out[s][:], in_=S[TILES * s : TILES * (s + 1)].rearrange("g f e -> f g e"))
 
-        for pair in range(G // 2):
-            res = sbuf("res%d" % pair, [P, 2, D], F32)
-            for h in range(2):
-                g = 2 * pair + h
-                nc.vector.scalar_tensor_tensor(out=res[:, h, :], in0=S_out[:, g, :], scalar=al_col[g],
-                                               in1=banks[divmod(g, TILES)][:, D : 2 * D],
+        for s in range(SETS):
+            kn_w = sbuf("kn_w%d" % s, [P, D, PACK], BF16)
+            cast(nc.scalar, kn_w[:], kn_raw[s][:])
+            u_w = sbuf("u_w%d" % s, [P, D, PACK], BF16)
+            cast(nc.vector, u_w[:], u_rows[s][:])
+            kn_q = quantize("kn%d" % s, kn_w)
+            u_q = quantize("u%d" % s, u_w)
+            for c in range(TILES):
+                product(banks[s, c][:, D : 2 * D], c, kn_q, u_q)
+
+        for first, count in ((0, 2), (2, 2), (4, 2), (6, 1), (7, 1)):
+            res = sbuf("res%d" % first, [P, count, D], F32)
+            for h in range(count):
+                g = first + h
+                s, c = divmod(g, TILES)
+                nc.vector.scalar_tensor_tensor(out=res[:, h, :], in0=S_out[s][:, c, :], scalar=al_col[g],
+                                               in1=banks[s, c][:, D : 2 * D],
                                                op0=ALU.mult, op1=ALU.subtract)
-            nc.sync.dma_start(out=out[2 * pair : 2 * pair + 2].rearrange("g f e -> f g e"), in_=res[:])
+            nc.sync.dma_start(out=out[first : first + count].rearrange("g f e -> f g e"), in_=res[:])

@@ -39,8 +39,8 @@ def tile_rows_upd_ttt_kernel(tc, kT, S, v, be, kn, al, out):
         def rows_of(x):
             return x.rearrange("(s c) (p j) n -> (c p) s (j n)", s=SETS, j=PACK)
 
-        def sbuf(name, shape, dtype):
-            return sb.tile(shape, dtype, name=name, align_bytes=64)
+        def sbuf(name, shape, dtype, tag=None):
+            return sb.tile(shape, dtype, name=name, tag=tag or name, align_bytes=64)
 
         def cast(engine, dst, src):
             o, i = interleaved(dst, src)
@@ -65,7 +65,7 @@ def tile_rows_upd_ttt_kernel(tc, kT, S, v, be, kn, al, out):
         small = sbuf("small_rows", [P, G * ROWS], F32)
         nc.vector.memset(small[:], 0.0)
 
-        kT_raw, S_raw, v_raw = [], [], []
+        kT_raw, S_raw = [], []
         for s in range(SETS):
             kT_raw.append(sbuf("kT_raw%d" % s, [P, PACK, D], F32))
             nc.sync.dma_start(out=kT_raw[s][:].rearrange("p j n -> p (j n)"), in_=rows_of(kT)[:, s, :])
@@ -75,12 +75,23 @@ def tile_rows_upd_ttt_kernel(tc, kT, S, v, be, kn, al, out):
                 for r, x in enumerate((be, al)):
                     nc.sync.dma_start(out=small[r:P:ROWS, :].rearrange("q (g r) -> q g r", g=G),
                                       in_=x.rearrange("g (q r) o -> q g (r o)", r=ROWS))
+        v_tok = {}
         for s in range(SETS):
-            v_raw.append(sbuf("v_raw%d" % s, [P, TILES, D], F32))
-            nc.sync.dma_start(out=v_raw[s][:], in_=v[TILES * s : TILES * (s + 1)].rearrange("g i e -> i g e"))
-        kn_raw = [sbuf("kn_raw%d" % s, [P, PACK, D], F32) for s in range(SETS)]
-        nc.sync.dma_start(out=kn_raw[0][:].rearrange("p j n -> p (j n)"), in_=rows_of(kn)[:, 0, :])
+            for c in range(2):
+                g = TILES * s + c
+                t = sbuf("v_tok%d" % g, [P, 2, D], F32)
+                nc.sync.dma_start(out=t[:], in_=v[g : g + 3 : 2].rearrange("g i e -> i g e"))
+                v_tok[g], v_tok[g + 2] = t[:, 0, :], t[:, 1, :]
 
+        S_out = {}
+
+        def load_state(first):
+            t = sbuf("S_out%d" % first, [P, 2, D], F32)
+            nc.sync.dma_start(out=t[:], in_=S[first : first + 2].rearrange("g f e -> f g e"))
+            for h in range(2):
+                S_out[first + h] = t[:, h, :]
+
+        load_state(0)
         banks = {}
         for s in range(SETS):
             for c in range(TILES):
@@ -100,31 +111,31 @@ def tile_rows_upd_ttt_kernel(tc, kT, S, v, be, kn, al, out):
                 product(banks[s, c][:, 0:D], c, kT_q, S_q)
             if s == 0:
                 nc.vector.transpose(out=cols[:], in_=small[:])
+                kn_raw = sbuf("kn_raw", [P, SETS, PACK * D], F32, tag="kT_raw0")
+                nc.gpsimd.dma_start(out=kn_raw[:], in_=rows_of(kn))
 
         u_rows = [sbuf("u_rows%d" % s, [P, PACK, D], BF16) for s in range(SETS)]
         for s in range(SETS):
             for c in ORDER:
                 g = TILES * s + c
                 vb = sbuf("vb%d" % g, [P, D], F32)
-                nc.scalar.activation(out=vb[:], in_=v_raw[s][:, c, :], func=COPY, scale=be_col[g])
+                nc.scalar.activation(out=vb[:], in_=v_tok[g], func=COPY, scale=be_col[g])
                 u_tok = sbuf("u_tok%d" % g, [P, D], BF16)
                 nc.vector.scalar_tensor_tensor(out=u_tok[:], in0=banks[s, c][:, 0:D], scalar=be_col[g],
                                                in1=vb[:], op0=ALU.mult, op1=ALU.subtract)
                 nc.sync.dma_start(out=u_rows[s][ROWS * c : ROWS * (c + 1)], in_=u_tok[:])
-            if s == 0:
-                nc.sync.dma_start(out=kn_raw[1][:].rearrange("p j n -> p (j n)"), in_=rows_of(kn)[:, 1, :])
 
-        S_out = []
-        for s in range(SETS):
-            S_out.append(sbuf("S_out%d" % s, [P, TILES, D], F32))
-            nc.sync.dma_start(out=S_out[s][:], in_=S[TILES * s : TILES * (s + 1)].rearrange("g f e -> f g e"))
+        for first in range(2, G, 2):
+            load_state(first)
 
+        kn_w = []
+        for s, engine in enumerate((nc.scalar, nc.vector)):
+            kn_w.append(sbuf("kn_w%d" % s, [P, D, PACK], BF16))
+            cast(engine, kn_w[s][:], kn_raw[:, s, :].rearrange("p (j n) -> p j n", j=PACK))
         for s in range(SETS):
-            kn_w = sbuf("kn_w%d" % s, [P, D, PACK], BF16)
-            cast(nc.scalar, kn_w[:], kn_raw[s][:])
             u_w = sbuf("u_w%d" % s, [P, D, PACK], BF16)
             cast(nc.vector, u_w[:], u_rows[s][:])
-            kn_q = quantize("kn%d" % s, kn_w)
+            kn_q = quantize("kn%d" % s, kn_w[s])
             u_q = quantize("u%d" % s, u_w)
             for c in range(TILES):
                 product(banks[s, c][:, D : 2 * D], c, kn_q, u_q)
@@ -134,7 +145,7 @@ def tile_rows_upd_ttt_kernel(tc, kT, S, v, be, kn, al, out):
             for h in range(count):
                 g = first + h
                 s, c = divmod(g, TILES)
-                nc.vector.scalar_tensor_tensor(out=res[:, h, :], in0=S_out[s][:, c, :], scalar=al_col[g],
+                nc.vector.scalar_tensor_tensor(out=res[:, h, :], in0=S_out[g], scalar=al_col[g],
                                                in1=banks[s, c][:, D : 2 * D],
                                                op0=ALU.mult, op1=ALU.subtract)
             nc.sync.dma_start(out=out[first : first + count].rearrange("g f e -> f g e"), in_=res[:])

from contextlib import ExitStack

import concourse.mybir as mybir

G, D = 8, 128
FLOPS = 2 * 2 * G * D * D * D

F32 = mybir.dt.float32
BF16 = mybir.dt.bfloat16
U32 = mybir.dt.uint32
U8 = mybir.dt.uint8
FP8X4 = mybir.dt.float8_e4m3fn_x4
ALU = mybir.AluOpType
COPY = mybir.ActivationFunctionType.Copy

P = 128
PACK = 4
ROWS = 32
TILES = 4
SETS = 2
RUN = 4
ORDER = (0, 2, 1, 3)


def interleaved(dst, src):
    return (
        dst.rearrange("p (c i) t -> p c t i", i=RUN),
        src.rearrange("p t (c i) -> p c t i", i=RUN),
    )


def tile_rows_upd_ttt_kernel(tc, kT, S, v, be, kn, al, out):
    nc = tc.nc
    with ExitStack() as ctx:
        sb = ctx.enter_context(tc.tile_pool(name="sb", bufs=1))
        ps = ctx.enter_context(tc.psum_pool(name="ps", bufs=1))
        ctx.enter_context(tc.manual_schedule())

        def rows_of(x):
            return x.rearrange("(s c) (p j) n -> (c p) s (j n)", s=SETS, j=PACK)

        def sbuf(name, shape, dtype, tag=None):
            return sb.tile(shape, dtype, name=name, tag=tag or name, align_bytes=64)

        def cast(engine, dst, src):
            o, i = interleaved(dst, src)
            if engine is nc.scalar:
                nc.scalar.activation(out=o, in_=i, func=COPY)
            else:
                nc.vector.tensor_copy(out=o, in_=i)

        def quantize(name, words):
            codes = sbuf(name + "_codes", [P, D], U32)
            scales = sbuf(name + "_scales", [P, D], U8)
            nc.vector.quantize_mx(out=codes[:].bitcast(FP8X4), scales=scales[:],
                                  in_=words[:].rearrange("p n j -> p (n j)"))
            return codes, scales

        def product(dst, c, lhs, rhs):
            r = slice(ROWS * c, ROWS * (c + 1))
            nc.tensor.matmul_mx(out=dst, lhsT=lhs[0][r, :].bitcast(FP8X4), lhsT_scale=lhs[1][r, :],
                                rhs=rhs[0][r, :].bitcast(FP8X4), rhs_scale=rhs[1][r, :],
                                start=True, stop=True)

        small = sbuf("small_rows", [P, G * ROWS], F32)
        nc.vector.memset(small[:], 0.0)

        kT_raw, S_raw = [], []
        for s in range(SETS):
            kT_raw.append(sbuf("kT_raw%d" % s, [P, PACK, D], F32))
            nc.sync.dma_start(out=kT_raw[s][:].rearrange("p j n -> p (j n)"), in_=rows_of(kT)[:, s, :])
            S_raw.append(sbuf("S_raw%d" % s, [P, PACK, D], F32))
            nc.sync.dma_start(out=S_raw[s][:].rearrange("p j n -> p (j n)"), in_=rows_of(S)[:, s, :])
            if s == 0:
                for r, x in enumerate((be, al)):
                    nc.sync.dma_start(out=small[r:P:ROWS, :].rearrange("q (g r) -> q g r", g=G),
                                      in_=x.rearrange("g (q r) o -> q g (r o)", r=ROWS))
        v_tok = {}
        for s in range(SETS):
            for c in range(2):
                g = TILES * s + c
                t = sbuf("v_tok%d" % g, [P, 2, D], F32)
                nc.sync.dma_start(out=t[:], in_=v[g : g + 3 : 2].rearrange("g i e -> i g e"))
                v_tok[g], v_tok[g + 2] = t[:, 0, :], t[:, 1, :]

        S_out = {}

        def load_state(first):
            t = sbuf("S_out%d" % first, [P, 2, D], F32)
            nc.sync.dma_start(out=t[:], in_=S[first : first + 2].rearrange("g f e -> f g e"))
            for h in range(2):
                S_out[first + h] = t[:, h, :]

        load_state(0)
        banks = {}
        for s in range(SETS):
            for c in range(TILES):
                banks[s, c] = ps.tile([P, 512], F32, name="bank%d%d" % (s, c))

        cols = sbuf("small_cols", [P, G * ROWS], F32)
        be_col = [cols[:, ROWS * g : ROWS * g + 1] for g in range(G)]
        al_col = [cols[:, ROWS * g + 1 : ROWS * g + 2] for g in range(G)]
        for s in range(SETS):
            kT_w = sbuf("kT_w%d" % s, [P, D, PACK], BF16)
            cast(nc.scalar, kT_w[:], kT_raw[s][:])
            S_w = sbuf("S_w%d" % s, [P, D, PACK], BF16)
            cast(nc.vector, S_w[:], S_raw[s][:])
            kT_q = quantize("kT%d" % s, kT_w)
            S_q = quantize("S%d" % s, S_w)
            for c in range(TILES):
                product(banks[s, c][:, 0:D], c, kT_q, S_q)
            if s == 0:
                nc.vector.transpose(out=cols[:], in_=small[:])
                kn_raw = sbuf("kn_raw", [P, SETS, PACK * D], F32, tag="kT_raw0")
                nc.gpsimd.dma_start(out=kn_raw[:], in_=rows_of(kn))

        u_rows = [sbuf("u_rows%d" % s, [P, PACK, D], BF16) for s in range(SETS)]
        for s in range(SETS):
            for c in ORDER:
                g = TILES * s + c
                vb = sbuf("vb%d" % g, [P, D], F32)
                nc.scalar.activation(out=vb[:], in_=v_tok[g], func=COPY, scale=be_col[g])
                u_tok = sbuf("u_tok%d" % g, [P, D], BF16)
                nc.vector.scalar_tensor_tensor(out=u_tok[:], in0=banks[s, c][:, 0:D], scalar=be_col[g],
                                               in1=vb[:], op0=ALU.mult, op1=ALU.subtract)
                nc.sync.dma_start(out=u_rows[s][ROWS * c : ROWS * (c + 1)], in_=u_tok[:])

        for first in range(2, G, 2):
            load_state(first)

        kn_w = []
        for s, engine in enumerate((nc.scalar, nc.vector)):
            kn_w.append(sbuf("kn_w%d" % s, [P, D, PACK], BF16))
            cast(engine, kn_w[s][:], kn_raw[:, s, :].rearrange("p (j n) -> p j n", j=PACK))
        for s in range(SETS):
            u_w = sbuf("u_w%d" % s, [P, D, PACK], BF16)
            cast(nc.vector, u_w[:], u_rows[s][:])
            kn_q = quantize("kn%d" % s, kn_w[s])
            u_q = quantize("u%d" % s, u_w)
            for c in range(TILES):
                product(banks[s, c][:, D : 2 * D], c, kn_q, u_q)

        for first, count in ((0, 2), (2, 2), (4, 2), (6, 1), (7, 1)):
            res = sbuf("res%d" % first, [P, count, D], F32)
            for h in range(count):
                g = first + h
                s, c = divmod(g, TILES)
                nc.vector.scalar_tensor_tensor(out=res[:, h, :], in0=S_out[g], scalar=al_col[g],
                                               in1=banks[s, c][:, D : 2 * D],
                                               op0=ALU.mult, op1=ALU.subtract)
            nc.sync.dma_start(out=out[first : first + count].rearrange("g f e -> f g e"), in_=res[:])
